import numpy as np, ml_dtypes
CORES = [3,11,19,27,35,43,51,59]
N = 8
BF = ml_dtypes.bfloat16
W, WX, I, B, SH = 4096, 3072, 192, 16, 12
DR, IR, GAP, RO = 5, 11, 3, 4
def parts(rng):
    mid = rng.choice(np.array([0.02, 0.05, 0.15, 0.4]), (N, 8, 1, 1)); e = rng.integers(0, 16, (N, 8, 16, WX)); small = (e * 5) >> 4
    x = np.where(rng.random((N, 8, 1, WX)) < mid, e, np.where(rng.random((N, 8, 1, WX)) < 0.5, small, 11 + small))
    g = np.minimum(np.maximum(rng.integers(1, 10, (N, 8, 1, I)) + rng.integers(-2, 3, (N, 8, 16, I)), 0), 15)
    g = np.where(rng.random((N, 8, 1, I)) < 0.1, rng.integers(0, 16, g.shape), g)
    return x, g, rng.integers(0, W * WX, (N, 8, 16, W)), rng.integers(0, W, (N, 8, 16, I)), rng.integers(0, WX, (N, 8, 16, I))
def pack(x, g, rel, nam, grd):
    return {"xc": np.ascontiguousarray(x.reshape(N, 128, WX)).astype(np.float32).astype(BF), "rel": np.ascontiguousarray(rel.reshape(N, 128, W)).astype(np.int32),
            "nam": np.ascontiguousarray(nam.reshape(N, 128, I)).astype(np.int32), "grd": np.ascontiguousarray(grd.reshape(N, 128, I)).astype(np.int32),
            "lim": np.ascontiguousarray(g.reshape(N, 128, I)).astype(np.float32).astype(BF)}
def setup_inputs(rng):
    return pack(*parts(rng))
def skew(rng, n, shape):
    ex = rng.choice(np.array([1, 3, 6], np.float32), (N, 8, 1, 1))
    return np.minimum((n * rng.random(shape, dtype=np.float32) ** ex).astype(np.int64), n - 1)
def setup_inputs_spread(rng):
    x = np.minimum((16 * rng.random((N, 8, 1, WX), dtype=np.float32) * rng.random((N, 8, 16, WX), dtype=np.float32)).astype(np.int64), 15)
    x = np.where(rng.random((N, 8, 1, WX)) < 0.5, 15 - x, x)
    g = np.minimum((16 * rng.random((N, 8, 1, I)) * rng.random((N, 8, 16, I))).astype(np.int64), 15)
    return pack(x, g, skew(rng, W, (N, 8, 16, W)) + W * skew(rng, WX, (N, 8, 16, W)), skew(rng, W, (N, 8, 16, I)), skew(rng, WX, (N, 8, 16, I)))
def atends(rng, hi, shape, share):
    u = rng.random(shape)
    return np.where(u < 0.5 * share, 0, np.where(u < share, hi, rng.integers(0, hi + 1, shape)))
def kinds(rng, n):
    m = rng.random((N, 8, 1, n)); e = rng.integers(0, 2, (N, 8, 16, n))
    return 15 * np.where(m < 0.25, 0, np.where(m < 0.5, 1, e))
def setup_inputs_ends(rng):
    x = kinds(rng, WX); g = kinds(rng, I); big = W * WX - 1
    u = rng.random((N, 8, 16, W)); two = rng.integers(0, 2, u.shape)
    rel = np.where(u < 0.35, 0, np.where(u < 0.7, big, np.where(u < 0.85, np.where(two == 1, W - 1, W * (WX - 1)), rng.integers(0, W * WX, u.shape))))
    nam = atends(rng, W - 1, (N, 8, 16, I), 0.75); grd = atends(rng, WX - 1, (N, 8, 16, I), 0.75)
    for c in (0, WX - 1):
        x[:, :, :, c] = 15 * rng.integers(0, 2, (N, 8, 16)); x[0, :, :, c] = 0; x[1, :, :, c] = 15; x[N - 1, :, :, c] = 15
    for q in (0, 1, N - 1): grd[q] = (WX - 1) * rng.integers(0, 2, (8, 16, I))
    for q in (1, N - 1):
        turn = (np.arange(16)[None, :, None] + rng.integers(0, 16, (8, 1, I))) & 15
        g[q] = np.where(turn < 8, 0, g[q]); g[q, 7, :, I - 1] = 0; g[q, 0, :, 0] = 0; g[q, 3, :8, I - 1] = 0; g[q, 3, 8:, I - 1] = 15
    for q in range(N):
        if 1 < q < N - 1 or q == 0: g[q, :, :, 0] = 15; g[q, :, :, I - 1] = 15; g[q, :, :, 1] = 0; g[q, :, :, I - 2] = 0
    x[1, 7, :, WX // 2] = 0; grd[1, 7, 15, I - 1] = WX // 2
    for q in range(N):
        rel[q, 7, 15, W - 1] = big; rel[q, 0, 0, 0] = big; rel[q, 7, 15, 0] = 0; nam[q, 0, 0, 0] = 0; nam[q, 7, 15, I - 1] = W - 1; nam[q, 7, 0, I - 1] = W - 1
    return pack(x, g, rel, nam, grd)
def setup_inputs_corners(rng):
    x, g, rel, nam, grd = parts(rng)
    g = rng.integers(0, 15 - GAP, (N, 8, 16, I)); ones = np.arange(16)[:, None]
    ty = np.array([(16, 0), (0, 16), (0, 0), (DR, 16 - DR), (DR - 1, 17 - DR), (0, IR - 1), (0, IR), (DR + 1, 0), (16 - IR, IR), (17 - IR, IR - 1), (DR, 0), (DR - 1, 0)])
    c = np.arange(WX) & (B - 1); which = np.where(c < 8, c, rng.integers(0, 12, (N, 8, WX)))
    over = ty[which, 0][:, :, None, :]; under = ty[which, 1][:, :, None, :]
    role = (ones * (2 * rng.integers(0, 8, (N, 8, 1, WX)) + 1) + rng.integers(0, 16, (N, 8, 1, WX))) & 15
    gg = np.repeat(g, B, axis=3); coin = rng.random(gg.shape) < 0.5
    v = np.where(role < over, np.where(coin, gg + GAP + 1, 15), np.where(role >= 16 - under, np.where(coin, gg, 0), np.where(coin, gg + 1, gg + GAP)))
    ca = (np.arange(I) + rng.integers(0, 10, (N, 8, 1, 1))) % 10; r = rng.integers(0, B, (N, 8, 16, I)); two = rng.integers(0, 2, (N, 8, 16, I))
    cs = np.where(ca == 1, 0, np.where(ca == 2, 1, np.where(ca == 3, 2, r)))
    cs = np.where(ca == 4, np.where(ones == 15, 2, 0), np.where(ca == 5, np.where(ones == 0, 2, two), cs))
    cs = np.where(ca == 6, 3 + (r & 3), np.where(ca == 7, two, np.where(ca == 8, np.where(ones == 15, 0, 1), cs)))
    col = B * np.arange(I) + cs
    for q in range(N):
        for w in range(8):
            o = rng.permutation(WX); x[q, w][:, o] = v[q, w]; grd[q, w] = o[col[q, w]]
    g = np.where(ca == 9, 15, g)
    l = np.arange(W); m = rng.integers(0, 5, rel.shape)
    rel = np.where(m == 0, l + W * np.minimum(l, WX - 1), np.where(m == 1, l + W * (rel >> SH), np.where(m == 2, (W - 1) * rng.integers(0, 2, rel.shape) + W * (WX - 1) * rng.integers(0, 2, rel.shape), rel)))
    nam = np.where(rng.random(nam.shape) < 0.3, (W - 1) * rng.integers(0, 2, nam.shape), nam)
    return pack(x, g, rel, nam, grd)
def setup_inputs_alike(rng):
    x, g, rel, nam, grd = parts(rng)
    grd[:, ::2] = rng.choice(np.array([0, WX - 1, WX // 2, 3]), (N, 4, 16, I)); grd[:, 1] = np.repeat(grd[:, 1, :1], 16, axis=1)
    nam[:, 2] = rng.choice(np.array([0, W - 1]), (N, 16, I)); nam[:, 3] = np.repeat(nam[:, 3, :1], 16, axis=1)
    rel[:, 5] = rng.choice(rng.integers(0, W * WX, 6), (N, 16, W)); rel[:, 7] = np.repeat(rel[:, 7, :1], 16, axis=1)
    x[:, 4] = 4 + GAP + rng.integers(0, 2, (N, 16, WX)); g[:, 4] = rng.choice(np.array([4, 4 + GAP]), (N, 16, I))
    x[N - 1, 4] = rng.integers(5, 5 + GAP, (16, WX)); g[N - 1, 4] = 4
    for q in range(N):
        c = int(rng.choice(np.array([0, WX - 1, WX // 2, 3]))); grd[q, 6] = c; x[q, 6, :, c] = rng.permutation(16)
        grd[q, 7] = rng.permutation(np.arange(16 * I) % WX).reshape(16, I)
    return pack(x, g, rel, nam, grd)
def check_inputs(d):
    bad = []
    for k, hi in (("xc", 15), ("rel", W * WX - 1), ("nam", W - 1), ("grd", WX - 1), ("lim", 15)):
        v = np.asarray(d[k]).astype(np.float64)
        if not (np.min(v) >= 0 and np.max(v) <= hi): bad.append("range of " + k)
        elif np.any(v != np.floor(v)): bad.append("whole numbers of " + k)
    return bad
def reference(xc, rel, nam, grd, lim):
    x = xc.astype(np.float32).astype(np.int32).reshape(N, 8, 16, WX); g = lim.astype(np.float32).astype(np.int32).reshape(N, 8, 16, I)
    tab = rel.reshape(N, 8, 16, W); a = nam.astype(np.int32).reshape(N, 8, 16, I); b = grd.astype(np.int32).reshape(N, 8, 16, I)
    deaths = np.zeros(N, np.int64); wt = (2 * np.arange(16) + 1)[None, :, None]
    for t in range(RO):
        for q in range(N):
            v = np.take_along_axis(x[q], b[q].reshape(8, 1, 16 * I), 2).reshape(8, 16, 16, I)
            gq = g[q][:, :, None, :]
            over = np.sum(v > gq + GAP, axis=1); under = np.sum(v <= gq, axis=1)
            dead = over >= DR + (deaths[q] & 1); imp = ~dead & (under >= IR); und = ~dead & ~imp
            some = np.any(und, axis=1); s = np.argmax(und, axis=1)
            z = np.where(dead, np.take_along_axis(a[q], s[:, None, :], 1), a[q])
            new = np.take_along_axis(tab[q], z, 2)
            vs = np.take_along_axis(v, s[:, None, None, :], 2)[:, :, 0]
            g[q] = np.where(some[:, None, :], np.maximum(g[q], vs), g[q])
            a[q] = np.where(und, a[q], new & (W - 1)); b[q] = np.where(und, b[q], new >> SH)
            deaths[q] = np.sum(dead)
        sent = np.array(g)
        for q in range(N):
            h = sent[(q - 1 - t % (N - 1)) % N]
            if t < RO - 1:
                place = B * np.arange(I) + (np.sum(wt * h, axis=1) & (B - 1))
                place = np.repeat(place[:, None, :], 16, axis=1)
                np.put_along_axis(x[q], place, (np.take_along_axis(x[q], place, 2) + h) >> 1, 2)
            g[q] = np.minimum(sent[q], h + 2)
    return {"yn": a.reshape(N, 128, I).astype(np.float32), "yg": b.reshape(N, 128, I).astype(np.float32), "yl": g.reshape(N, 128, I).astype(np.float32).astype(BF)}

@@ -1,0 +1,324 @@
+import numpy as np
+from concourse.mybir import AluOpType, ActivationFunctionType
+
+A = AluOpType
+F = ActivationFunctionType
+RO = 4
+NS = 192
+NL = 3072
+PAD = 3072
+BIAS = 130
+TOP = 12582912
+CH = [(0, 64), (64, 128), (128, 192)]
+LAST = len(CH) - 1
+SCAN = 2
+C0 = CH[SCAN][0] if SCAN <= LAST else NS
+G_LANES, V_LANES = 3, 4
+
+SCRATCH = {}
+
+
+def _buf(where, dtype, **names):
+    for name, cols in names.items(): SCRATCH[name] = (where, [128, cols], dtype)
+
+
+_buf("sbuf", "bfloat16", gl=NS, xr=NL, xb=NL, gx=NL, D=2 * NL, ob=NL, ub=NL, yo=NS, dead=NS, und=NS, imp=NS, fi=NS, tr=NS, gm=NS, r16=16, tx=NS, half=NS,
+     cs=NS, zo=144, zl=144, zq=144, idn=128, idm=128, id64=128, idq=128, idr=128, y1=128, y2=128, y3=128, ym=128, zz=128, one=NS, base=12)
+_buf("sbuf", "float32", mf=4096, W=2 * NL, sc=NL, hold=NL, h16=16, h17=16, kf=NS, lf=NS, t1=NS, t3=NS, t4=NS, hh=NS, cf=1, th=1, jm=144, ln=16, kc=1, bc=12,
+     b3=12, x1=12, x2=12, c15=1, c16=1, e15=1, me=1, w1=1, wl=1, wq=1, q1=1, q2=1, q3=1, k1=1, sv1=1, ek=2048, kt=1)
+_buf("sbuf", "int32", gi=NS, ni=NS, mi=4096, ci=NS, k32=NS, l32=NS, c32=1, c33=1, pi=1, ka=1)
+_buf("sbuf", "uint16", ku=NS, lu=NS, idx=16, li=16)
+_buf("psum", "float32", PU=512, PO=512, PY=512, PL=512, PA=512, PQ=512, PC=512, PG=512)
+for _t in range(RO): _buf("sbuf", "bfloat16", **{"gs%d" % _t: NS, "h%d" % _t: NS})
+NDMA = 11
+SEMAPHORES = ["sv", "ss", "sp", "sg", "snt"] + ["arr%d" % t for t in range(RO)] + ["dm%d" % i for i in range(NDMA)]
+
+
+def rank_program(g, core, T, topo):
+    rank = T.rank_of(core)
+    if rank is None:
+        return
+    cores = list(T.cores)
+    n = len(cores)
+    S = T.sem
+    queues = {"v": (g.vector, "sv"), "s": (g.scalar, "ss"), "p": (g.tensor, "sp"), "g": (g, "sg"), "y": (g.sync, None)}
+    count = {"sv": 0, "ss": 0, "sp": 0, "sg": 0}
+    seen = {}
+    log = {}
+
+    def need(q, sem, val):
+        if seen.get((q, sem), 0) < val:
+            queues[q][0].wait_ge(S[sem], val)
+            seen[(q, sem)] = val
+
+    def prep(q, reads, writes):
+        todo = {}
+        for wr, regs in ((False, reads), (True, writes)):
+            for name, lo, hi in regs:
+                bank = name in SCRATCH and SCRATCH[name][0] == "psum"
+                for (w0, l0, h0, q0, sem0, val0) in log.get(name, []):
+                    over = l0 < hi and lo < h0
+                    if q0 == q: hit = (w0 or wr) and over and not (q == "p" and bank)
+                    elif bank: hit = True
+                    else: hit = (w0 or wr) and over
+                    if hit: todo[sem0] = max(todo.get(sem0, 0), val0)
+        for sem0 in sorted(todo): need(q, sem0, todo[sem0])
+
+    def note(q, sem, val, reads, writes):
+        for wr, regs in ((False, reads), (True, writes)):
+            for name, lo, hi in regs:
+                old = log.setdefault(name, [])
+                old[:] = [e for e in old if not (lo <= e[1] and e[2] <= hi and (wr or (not e[0] and e[3] == q and e[4] == sem)))]
+                old.append((wr, lo, hi, q, sem, val))
+
+    def op(q, fn, reads, writes):
+        prep(q, reads, writes)
+        sem = queues[q][1]
+        fn(queues[q][0]).then_inc(S[sem], 1)
+        count[sem] += 1
+        note(q, sem, count[sem], reads, writes)
+
+    dmas = [0]
+
+    def dma(q, out, in_, reads, writes):
+        prep(q, reads, writes)
+        sem = "dm%d" % dmas[0]
+        dmas[0] += 1
+        queues[q][0].dma_start(out, in_).then_inc(S[sem], 16)
+        note("dma", sem, 16, reads, writes)
+
+    def R(name, lo=0, hi=None): return (name, lo, SCRATCH[name][1][1] if hi is None and name in SCRATCH else hi)
+
+    def V(name, lo=0, hi=None):
+        r = R(name, lo, hi)
+        return (T[name][:, r[1]:r[2]], [r])
+
+    def step(name, lo, hi, first):
+        return (T[name][:, lo + first:hi:16], [R(name, lo, hi)])
+
+    def at(win, lst):
+        return (win[0].indirect(lst[0]), win[1] + lst[1])
+
+    def ts(out, in0, s1, op0, s2=None, op1=None):
+        reads = list(in0[1])
+        a, b = s1, s2
+        if isinstance(s1, str): a, reads = T[s1][:], reads + [R(s1)]
+        if isinstance(s2, str): b, reads = T[s2][:], reads + [R(s2)]
+        if op1 is None: op("v", lambda v: v.tensor_scalar(out[0], in0[0], a, None, op0), reads, out[1])
+        else: op("v", lambda v: v.tensor_scalar(out[0], in0[0], a, b, op0, op1), reads, out[1])
+
+    def tt(out, a, b, f, lists=()): op("v", lambda v: v.tensor_tensor(out[0], a[0], b[0], f), a[1] + b[1] + list(lists), out[1])
+
+    def cp(out, a): op("v", lambda v: v.tensor_copy(out[0], a[0]), a[1], out[1])
+
+    def fill(out, c): op("v", lambda v: v.memset(out[0], c), [], out[1])
+
+    def act(out, a, func=F.Identity, bias=0.0, scale=1.0): op("s", lambda s: s.activation(out[0], a[0], func, bias=bias, scale=scale), a[1], out[1])
+
+    def mm(out, lhsT, rhs, start, stop): op("p", lambda p: p.matmul(out[0], lhsT[0], rhs[0], start, stop), lhsT[1] + rhs[1], out[1])
+
+    def slide(name, k): return (T[name][:, 15 - k:143 - k], [R(name)])
+
+    def lane_gx(q, k, src):
+        o = T.gx[:, k::16]
+        w = [("gx%d" % k, 0, NL)]
+        if q == "v": op("v", lambda v: v.tensor_copy(o, src[0]), src[1], w)
+        elif q == "s": op("s", lambda s: s.activation(o, src[0], F.Identity), src[1], w)
+        else: op("g", lambda q: q.affine_select(o, src[0], [[0, NS]], A.is_gt, 0.0, 1, 0), src[1], w)
+
+    GV = list(range(V_LANES))
+    GG = list(range(V_LANES, V_LANES + G_LANES))
+    GS = list(range(V_LANES + G_LANES, 16))
+
+    dma("y", T.gl[:], T.lim[:], [], [R("gl")])
+    dma("y", T.gi[:], T.grd[:], [], [R("gi")])
+    dma("y", T.ni[:], T.nam[:], [], [R("ni")])
+    dma("y", T.xr[:], T.xc[:], [], [R("xr")])
+    QM = [(1024 * b, 1024 * b + 1024) for b in range(4)]
+    for lo, hi in QM: dma("y", T.mi[:, lo:hi], T.rel[:, lo:hi], [], [R("mi", lo, hi)])
+
+    IMP = {"allow_small_or_imprecise_dtypes": True}
+    op("g", lambda q: q.iota(T.jm[:], [[1, 144]], 0, -1, **IMP), [], [R("jm")])
+    op("g", lambda q: q.iota(T.pi[:], [[1, 1]], 0, 1), [], [R("pi")])
+    op("g", lambda q: q.iota(T.bc[:], [[256, 12]], 0, 0, **IMP), [], [R("bc")])
+    op("g", lambda q: q.iota(T.ln[:], [[1, 16]], 0, 0, **IMP), [], [R("ln")])
+    op("g", lambda q: q.iota(T.ek[:], [[1000, 16], [1, 128]], 0, -1, **IMP), [], [R("ek")])
+    for k in GG: lane_gx("g", k, V("gl"))
+    for lo, hi in QM: op("g", lambda q: q.affine_select(T.mf[:, lo:hi], T.mi[:, lo:hi], [[0, 1024]], A.is_gt, 0.0, 1, 0), [R("mi", lo, hi)], [R("mf", lo, hi)])
+    jm = V("jm", 0, 128)
+    ts(V("ka"), V("pi"), 15, A.bitwise_and)
+    cp(V("kc"), V("ka"))
+    ts(V("c15"), V("kc"), -1.0, A.mult, 15.0, A.add)
+    ts(V("zo"), V("jm"), "c15", A.is_equal)
+    cp(V("ku"), V("gi"))
+    fill(V("zz"), 0.0)
+    for k in GV: lane_gx("v", k, V("gl"))
+    for k in GS: lane_gx("s", k, V("gl"))
+    act(V("PG", 0, NS), V("gl"), bias=float(BIAS))
+    for j in range(NL // NS): act(V("W", PAD + NS * j, PAD + NS * j + NS), V("gl"))
+    ts(V("e15"), V("kc"), 15.0, A.is_equal)
+    ts(V("c16"), V("c15"), 1.0, A.add)
+    ts(V("me"), V("e15"), -1.0, A.mult)
+    ts(V("w1"), V("e15"), float(PAD), A.mult)
+    tt(V("wl"), V("w1"), V("c15"), A.subtract)
+    ts(V("zl"), V("jm"), "c15", A.is_equal, "wl", A.mult)
+    ts(V("idn"), jm, 0.0, A.is_equal)
+    ts(V("id64"), jm, 0.0, A.is_equal, 64.0, A.mult)
+    ts(V("y1"), jm, 0.0, A.is_gt)
+    ts(V("y2"), jm, "c16", A.is_lt)
+    tt(V("y3"), V("y1"), V("y2"), A.mult)
+    ts(V("y1"), jm, 0.0, A.is_equal, "e15", A.mult)
+    ts(V("y1"), V("y1"), -2.0, A.mult)
+    tt(V("y2"), V("idn"), V("y1"), A.add)
+    tt(V("ym"), V("y2"), V("y3"), A.subtract)
+    ts(V("q1"), V("kc"), 16.0, A.mult)
+    ts(V("base"), V("bc"), "q1", A.add)
+
+    def late_constants():
+        ts(V("idm"), jm, 0.0, A.is_equal, -1.0, A.mult)
+        fill(V("one"), 1.0)
+        ts(V("k32"), V("gi"), 4096.0, A.mult, float(-TOP), A.add)
+        tt(V("ci"), V("k32"), V("ni"), A.add)
+        cp(V("lu"), V("ni"))
+        ts(V("k1"), V("kc"), 1.0, A.add)
+        ts(V("h16"), V("ln"), "k1", A.is_equal, 16777215.0, A.mult)
+        ts(V("h17"), V("ln"), "kc", A.is_gt)
+        tt(V("hold", 16 * C0, 16 * C0 + 16), V("h16"), V("h17"), A.add) if C0 < NS else None
+        ts(V("sv1"), V("e15"), 2.0 ** 24 - 1.0, A.mult, 1.0, A.add)
+        ts(V("sv1"), V("sv1"), 2.0 ** -24, A.mult)
+        ts(V("idq"), jm, 0.0, A.is_equal, "sv1", A.mult)
+        ts(V("idr"), V("idq"), -1.0, A.mult)
+        ts(V("kt"), V("kc"), 1000.0, A.mult)
+        ts(V("ek"), V("ek"), "kt", A.is_equal)
+        ts(V("q1"), V("kc"), 8.0, A.is_ge, -16.0, A.mult)
+        ts(V("q2"), V("kc"), 2.0, A.mult, 1.0, A.add)
+        tt(V("q2"), V("q2"), V("q1"), A.add)
+        ts(V("q1"), V("q2"), 8.0, A.is_ge, -16.0, A.mult)
+        tt(V("wq"), V("q2"), V("q1"), A.add)
+        ts(V("zq"), V("jm"), "c15", A.is_equal, "wq", A.mult)
+        ts(V("b3"), V("base"), 3072.0, A.add)
+        fill(V("half"), 0.5)
+
+    def spread_hold():
+        w, base = 16, 16 * C0
+        while base + w < NL:
+            m = min(w, NL - base - w)
+            act(V("hold", base + w, base + w + m), V("hold", base, base + m))
+            w += m
+
+    def gather_w(q, c):
+        a, b = CH[c]
+        out, src = V("W", 16 * a, 16 * b), at(V("mf"), V("lu", a, b))
+        pad, first = (T.W[:, PAD + 15 + 16 * a:PAD + 16 * b:16], [R("W", PAD + 16 * a, PAD + 16 * b)]), step("W", 16 * a, 16 * b, 0)
+        if q == "s":
+            act(out, src, bias=float(-TOP))
+            act(pad, first)
+        else:
+            ts(out, src, float(-TOP), A.add)
+            cp(pad, first)
+
+    def diag(c):
+        a, b = CH[c]
+        for k in range(16): mm(V("PA", a, b), V("ek", 128 * k, 128 * k + 128), step("W", 16 * a, 16 * b, k), k == 0, k == 15)
+
+    def tally(dst, src, c, alone):
+        a, b = CH[c]
+        for k in range(16): mm(V(dst, a, b), slide("zo", k), step(src, 16 * a, 16 * b, k), alone and k == 0, alone and k == 15)
+
+    for t in range(RO):
+        X = V("xr") if t == 0 else V("xb")
+        gs, h = "gs%d" % t, "h%d" % t
+        mm(V("PU", 0, NS), V("zz"), V("gl"), True, False)
+        for c, (a, b) in enumerate(CH):
+            p = (16 * a, 16 * b)
+            tt(V("D", *p), at(X, V("ku", a, b)), (T.gx[:, p[0]:p[1]], [("gx%d" % k, 0, NL) for k in range(16)]), A.subtract)
+            ts(V("ob", *p), V("D", *p), 3.5, A.is_gt)
+            act(V("ub", *p), V("D", *p), F.Sign, bias=0.5, scale=-1.0)
+            if t > 0 and c < LAST: gather_w("s", c)
+            tally("PO", "ob", c, True)
+            if c == 0 and t > 0: act(V("PG", 0, NS), V("gm"), bias=2.0)
+            if c == LAST and t > 0:
+                cp(V("c32"), V("cf"))
+                ts(V("c33"), V("c32"), 1, A.bitwise_and)
+                ts(V("th"), V("c33"), 5.0, A.add)
+            if c == LAST and t == 0: fill(V("D", PAD, PAD + 1280), 0.0)
+            if c == LAST: ts(V("dead"), V("PO", 0, NS), "th" if t else 5.0, A.is_ge)
+            if c == LAST and t == 0: fill(V("D", PAD + 1280, PAD + 2176), 0.0)
+            tally("PU", "ub", c, False)
+            if c == 0 and t > 0 and c < SCAN: diag(0)
+        mm(V("PU", 0, NS), V("id64"), V("dead"), False, True)
+        ts(V("und"), V("PU", 0, NS), 5.0, A.is_lt)
+        if t == 0: fill(V("D", PAD + 2176, 2 * NL), 0.0)
+        mm(V("PL", 0, 12), V("idn"), V("base"), True, False)
+        mm(V("PY", 0, NS), V("ym"), V("und"), True, True)
+        ts(V("fi"), V("PY", 0, NS), "me", A.max, "e15", A.add)
+        for k in range(16): mm(V("PL", 0, 12), slide("zl", k), step("fi", 0, NS, k), False, k == 15)
+        ts(V("idx", 0, 12), V("PL", 0, 12), 15.0, A.add)
+        ts(V("tr"), at(V("D"), V("idx", 0, 12)), 0.0, A.max)
+        tt(V(gs), V("PG", 0, NS), V("tr"), A.add)
+        dst, src = cores[(rank + 1 + t % (n - 1)) % n], cores[(rank - 1 - t % (n - 1)) % n]
+        rid, pid, _ = topo.addr(dst)
+        prep("g", [R(gs)], [])
+        g.remote_dma(T[h][:], T[gs][:], S["arr%d" % t], S.snt, pid, rid, topo.mask(core, dst))
+        note("remote", "arr%d" % t, len(topo.engines(src, core)), [], [R(h)])
+        if t == 0:
+            late_constants()
+            act(V("xb"), V("xr"), bias=128.0)
+            spread_hold()
+        else: gather_w("s", LAST)
+        mm(V("PY", 256, 256 + NS), V("idn"), V("und"), True, True)
+        for lo, hi, pos, neg in ((0, C0, "idn", "idm"), (C0, NS, "idq", "idr")):
+            if lo < hi:
+                o = V("PC", 256 + lo, 256 + hi)
+                mm(o, V(pos), V("one", lo, hi), True, False)
+                mm(o, V(neg), V("und", lo, hi), False, False)
+                mm(o, V(neg), V("dead", lo, hi), False, True)
+        act(V("imp"), V("PC", 256, 256 + NS))
+        act(V("PG", 256, 256 + NS), V(gs), bias=-2.0)
+        if t == 0:
+            for c in range(LAST): gather_w("s", c)
+            gather_w("v", LAST)
+        for c in range(0 if t == 0 else 1, min(SCAN, LAST + 1)): diag(c)
+        if t < RO - 1:
+            mm(V("PC", 0, NS), V("one", 0, 128), V("dead"), True, True)
+            op("s", lambda s: s.activation(T.cs[:], T.PC[:, 0:NS], F.Identity, accum_out=T.cf[:]), [R("PC", 0, NS)], [R("cs"), R("cf")])
+        tt(V("t3"), V("PY", 256, 256 + NS), V("ci"), A.mult)
+        if C0 < NS:
+            p = (16 * C0, NL)
+            op("v", lambda v: v.tensor_tensor_scan(T.sc[:, p[0]:p[1]], T.hold[:, p[0]:p[1]], T.W[:, p[0]:p[1]], 0.0, A.mult, A.min), [R("hold", *p), R("W", *p)], [R("sc", *p)])
+        tt(V("t1"), at(V("W"), V("idx", 0, 12)), V("dead"), A.mult)
+        tt(V("t4"), V("t1"), V("t3"), A.add)
+        if C0 < NS: tt(V("PA", 256 + C0, 256 + NS), step("sc", 16 * C0, NL, 15), V("imp", C0, NS), A.mult)
+        if C0 > 0: tt(V("PA", 256, 256 + C0), V("PA", 0, C0), V("imp", 0, C0), A.mult)
+        tt(V("ci"), V("PA", 256, 256 + NS), V("t4"), A.add)
+        ts(V("k32"), V("ci"), 12, A.arith_shift_right)
+        if t == RO - 1:
+            ts(V("l32"), V("ci"), 4095, A.bitwise_and)
+            ts(V("kf"), V("k32"), 3072.0, A.add)
+            dma("y", T.yg[:], T.kf[:], [R("kf")], [])
+            cp(V("lf"), V("l32"))
+            dma("y", T.yn[:], T.lf[:], [R("lf")], [])
+            tt(V("gm"), V("PG", 256, 256 + NS), V(h), A.min)
+            ts(V("yo"), V("gm"), float(2 - BIAS), A.add)
+            dma("y", T.yl[:], T.yo[:], [R("yo")], [])
+            break
+        ts(V("ku"), V("k32"), 3072.0, A.add)
+        tt(V("gm"), V("PG", 256, 256 + NS), V(h), A.min)
+        act(V("hh"), V(h), bias=127.5 - BIAS)
+        for k in range(16): mm(V("PQ", 0, 12), slide("zq", k), step(h, 0, NS, k), k == 0, k == 15)
+        for k in GG: lane_gx("g", k, V("gm"))
+        for k in GS: lane_gx("s", k, V("gm"))
+        ts(V("l32"), V("ci"), 4095, A.bitwise_and)
+        ts(V("r16", 0, 12), V("PQ", 0, 12), 3064.5, A.add)
+        tt(V("x1"), V("PQ", 0, 12), V("r16", 0, 12), A.subtract)
+        tt(V("x2"), V("x1"), V("b3"), A.add)
+        cp(V("li", 0, 12), V("x2"))
+        tt(V("tx"), at(V("xb"), V("li", 0, 12)), V("hh"), A.add)
+        cp(V("lu"), V("l32"))
+        for k in GV: lane_gx("v", k, V("gm"))
+        out = at(V("xb"), V("li", 0, 12))
+        tt((out[0], [R("xb")]), V("tx"), V("half"), A.mult, lists=[R("li", 0, 12)])
+
+    g.wait_ge(S.snt, sum(len(topo.engines(core, cores[(rank + 1 + t % (n - 1)) % n])) for t in range(RO)))
+    for sem in ("sv", "ss", "sp", "sg"): need("g", sem, count[sem])
+    for i in range(dmas[0]): need("g", "dm%d" % i, 16)

@@ -11,9 +11,7 @@ BIAS = 130
 TOP = 12582912
 CH = [(0, 64), (64, 128), (128, 192)]
 LAST = len(CH) - 1
-SCAN = 2
-C0 = CH[SCAN][0] if SCAN <= LAST else NS
-G_LANES, V_LANES = 3, 4
+G_LANES, V_LANES = 4, 3
 
 SCRATCH = {}
 
@@ -24,8 +22,8 @@ def _buf(where, dtype, **names):
 
 _buf("sbuf", "bfloat16", gl=NS, xr=NL, xb=NL, gx=NL, D=2 * NL, ob=NL, ub=NL, yo=NS, dead=NS, und=NS, imp=NS, fi=NS, tr=NS, gm=NS, r16=16, tx=NS, half=NS,
      cs=NS, zo=144, zl=144, zq=144, idn=128, idm=128, id64=128, idq=128, idr=128, y1=128, y2=128, y3=128, ym=128, zz=128, one=NS, base=12)
-_buf("sbuf", "float32", mf=4096, W=2 * NL, sc=NL, hold=NL, h16=16, h17=16, kf=NS, lf=NS, t1=NS, t3=NS, t4=NS, hh=NS, cf=1, th=1, jm=144, ln=16, kc=1, bc=12,
-     b3=12, x1=12, x2=12, c15=1, c16=1, e15=1, me=1, w1=1, wl=1, wq=1, q1=1, q2=1, q3=1, k1=1, sv1=1, ek=2048, kt=1)
+_buf("sbuf", "float32", mf=4096, W=2 * NL, sc=NL, hold=NL, h16=16, h17=16, kf=NS, lf=NS, t1=NS, t4=NS, hh=NS, cf=1, th=1, jm=144, ln=16, kc=1, bc=12,
+     b3=12, x1=12, x2=12, c15=1, c16=1, e15=1, me=1, w1=1, wl=1, wq=1, q1=1, q2=1, q3=1, k1=1, sv1=1, ek=2048, on16=16)
 _buf("sbuf", "int32", gi=NS, ni=NS, mi=4096, ci=NS, k32=NS, l32=NS, c32=1, c33=1, pi=1, ka=1)
 _buf("sbuf", "uint16", ku=NS, lu=NS, idx=16, li=16)
 _buf("psum", "float32", PU=512, PO=512, PY=512, PL=512, PA=512, PQ=512, PC=512, PG=512)
@@ -138,12 +136,16 @@ def rank_program(g, core, T, topo):
     for lo, hi in QM: dma("y", T.mi[:, lo:hi], T.rel[:, lo:hi], [], [R("mi", lo, hi)])
 
     IMP = {"allow_small_or_imprecise_dtypes": True}
+    fill(V("on16"), 1.0)
     op("g", lambda q: q.iota(T.jm[:], [[1, 144]], 0, -1, **IMP), [], [R("jm")])
     op("g", lambda q: q.iota(T.pi[:], [[1, 1]], 0, 1), [], [R("pi")])
     op("g", lambda q: q.iota(T.bc[:], [[256, 12]], 0, 0, **IMP), [], [R("bc")])
     op("g", lambda q: q.iota(T.ln[:], [[1, 16]], 0, 0, **IMP), [], [R("ln")])
-    op("g", lambda q: q.iota(T.ek[:], [[1000, 16], [1, 128]], 0, -1, **IMP), [], [R("ek")])
     for k in GG: lane_gx("g", k, V("gl"))
+    op("g", lambda q: q.iota(T.ek[:], [[0, 2048]], 0, 0, **IMP), [], [R("ek")])
+    for j in range(8):
+        o = T.ek[:, 16 * j:16 * j + 1936:129]
+        op("g", lambda q: q.affine_select(o, T.on16[:], [[-1, 16]], A.is_equal, 0.0, -16 * j, 1), [R("on16")], [R("ek")])
     for lo, hi in QM: op("g", lambda q: q.affine_select(T.mf[:, lo:hi], T.mi[:, lo:hi], [[0, 1024]], A.is_gt, 0.0, 1, 0), [R("mi", lo, hi)], [R("mf", lo, hi)])
     jm = V("jm", 0, 128)
     ts(V("ka"), V("pi"), 15, A.bitwise_and)
@@ -152,10 +154,16 @@ def rank_program(g, core, T, topo):
     ts(V("zo"), V("jm"), "c15", A.is_equal)
     cp(V("ku"), V("gi"))
     fill(V("zz"), 0.0)
+    ts(V("k1"), V("kc"), 1.0, A.add)
+    ts(V("h16"), V("ln"), "k1", A.is_equal, 16777215.0, A.mult)
+    ts(V("h17"), V("ln"), "kc", A.is_gt)
+    tt(V("hold", 0, 16), V("h16"), V("h17"), A.add)
+    cp(V("lu"), V("ni"))
     for k in GV: lane_gx("v", k, V("gl"))
     for k in GS: lane_gx("s", k, V("gl"))
     act(V("PG", 0, NS), V("gl"), bias=float(BIAS))
     for j in range(NL // NS): act(V("W", PAD + NS * j, PAD + NS * j + NS), V("gl"))
+    act(V("D", PAD, 2 * NL), V("xr"), scale=0.0)
     ts(V("e15"), V("kc"), 15.0, A.is_equal)
     ts(V("c16"), V("c15"), 1.0, A.add)
     ts(V("me"), V("e15"), -1.0, A.mult)
@@ -174,22 +182,21 @@ def rank_program(g, core, T, topo):
     ts(V("q1"), V("kc"), 16.0, A.mult)
     ts(V("base"), V("bc"), "q1", A.add)
 
-    def late_constants():
-        ts(V("idm"), jm, 0.0, A.is_equal, -1.0, A.mult)
-        fill(V("one"), 1.0)
-        ts(V("k32"), V("gi"), 4096.0, A.mult, float(-TOP), A.add)
-        tt(V("ci"), V("k32"), V("ni"), A.add)
-        cp(V("lu"), V("ni"))
-        ts(V("k1"), V("kc"), 1.0, A.add)
-        ts(V("h16"), V("ln"), "k1", A.is_equal, 16777215.0, A.mult)
-        ts(V("h17"), V("ln"), "kc", A.is_gt)
-        tt(V("hold", 16 * C0, 16 * C0 + 16), V("h16"), V("h17"), A.add) if C0 < NS else None
+    def constants_a():
         ts(V("sv1"), V("e15"), 2.0 ** 24 - 1.0, A.mult, 1.0, A.add)
         ts(V("sv1"), V("sv1"), 2.0 ** -24, A.mult)
+        ts(V("idm"), jm, 0.0, A.is_equal, -1.0, A.mult)
         ts(V("idq"), jm, 0.0, A.is_equal, "sv1", A.mult)
         ts(V("idr"), V("idq"), -1.0, A.mult)
-        ts(V("kt"), V("kc"), 1000.0, A.mult)
-        ts(V("ek"), V("ek"), "kt", A.is_equal)
+
+    def constants_b():
+        fill(V("one"), 1.0)
+        ts(V("k32"), V("gi"), 4096.0, A.mult, float(-TOP), A.add)
+
+    def constants_c():
+        tt(V("ci"), V("k32"), V("ni"), A.add)
+
+    def constants_d():
         ts(V("q1"), V("kc"), 8.0, A.is_ge, -16.0, A.mult)
         ts(V("q2"), V("kc"), 2.0, A.mult, 1.0, A.add)
         tt(V("q2"), V("q2"), V("q1"), A.add)
@@ -200,15 +207,14 @@ def rank_program(g, core, T, topo):
         fill(V("half"), 0.5)
 
     def spread_hold():
-        w, base = 16, 16 * C0
-        while base + w < NL:
-            m = min(w, NL - base - w)
-            act(V("hold", base + w, base + w + m), V("hold", base, base + m))
-            w += m
+        for w in (16, 32, 64, 128, 256, 512): act(V("hold", w, 2 * w), V("hold", 0, w))
+
+    def scan(lo, hi):
+        op("v", lambda v: v.tensor_tensor_scan(T.sc[:, lo:hi], T.hold[:, 0:hi - lo], T.W[:, lo:hi], 0.0, A.mult, A.min), [R("hold", 0, hi - lo), R("W", lo, hi)], [R("sc", lo, hi)])
 
     def gather_w(q, c):
         a, b = CH[c]
-        out, src = V("W", 16 * a, 16 * b), at(V("mf"), V("lu", a, b))
+        out, src = V("W", 16 * a, 16 * b), at(V("mf" if q == "s" else "mi"), V("lu", a, b))
         pad, first = (T.W[:, PAD + 15 + 16 * a:PAD + 16 * b:16], [R("W", PAD + 16 * a, PAD + 16 * b)]), step("W", 16 * a, 16 * b, 0)
         if q == "s":
             act(out, src, bias=float(-TOP))
@@ -233,26 +239,27 @@ def rank_program(g, core, T, topo):
             p = (16 * a, 16 * b)
             tt(V("D", *p), at(X, V("ku", a, b)), (T.gx[:, p[0]:p[1]], [("gx%d" % k, 0, NL) for k in range(16)]), A.subtract)
             ts(V("ob", *p), V("D", *p), 3.5, A.is_gt)
-            act(V("ub", *p), V("D", *p), F.Sign, bias=0.5, scale=-1.0)
             if t > 0 and c < LAST: gather_w("s", c)
+            act(V("ub", *p), V("D", *p), F.Sign, bias=0.5, scale=-1.0)
             tally("PO", "ob", c, True)
-            if c == 0 and t > 0: act(V("PG", 0, NS), V("gm"), bias=2.0)
+            if c == LAST and t > 0: act(V("PG", 0, NS), V("gm"), bias=2.0 if t < RO - 1 else 2.0 - 128)
             if c == LAST and t > 0:
                 cp(V("c32"), V("cf"))
                 ts(V("c33"), V("c32"), 1, A.bitwise_and)
                 ts(V("th"), V("c33"), 5.0, A.add)
-            if c == LAST and t == 0: fill(V("D", PAD, PAD + 1280), 0.0)
+            if c == LAST and t == 0: constants_a()
+            if c == LAST and t > 0: scan(0, 512)
             if c == LAST: ts(V("dead"), V("PO", 0, NS), "th" if t else 5.0, A.is_ge)
-            if c == LAST and t == 0: fill(V("D", PAD + 1280, PAD + 2176), 0.0)
+            if c == LAST and t == 0: constants_b()
             tally("PU", "ub", c, False)
-            if c == 0 and t > 0 and c < SCAN: diag(0)
         mm(V("PU", 0, NS), V("id64"), V("dead"), False, True)
         ts(V("und"), V("PU", 0, NS), 5.0, A.is_lt)
-        if t == 0: fill(V("D", PAD + 2176, 2 * NL), 0.0)
         mm(V("PL", 0, 12), V("idn"), V("base"), True, False)
         mm(V("PY", 0, NS), V("ym"), V("und"), True, True)
         ts(V("fi"), V("PY", 0, NS), "me", A.max, "e15", A.add)
+        if t == 0: constants_c()
         for k in range(16): mm(V("PL", 0, 12), slide("zl", k), step("fi", 0, NS, k), False, k == 15)
+        if t > 0: scan(512, 1024)
         ts(V("idx", 0, 12), V("PL", 0, 12), 15.0, A.add)
         ts(V("tr"), at(V("D"), V("idx", 0, 12)), 0.0, A.max)
         tt(V(gs), V("PG", 0, NS), V("tr"), A.add)
@@ -262,34 +269,33 @@ def rank_program(g, core, T, topo):
         g.remote_dma(T[h][:], T[gs][:], S["arr%d" % t], S.snt, pid, rid, topo.mask(core, dst))
         note("remote", "arr%d" % t, len(topo.engines(src, core)), [], [R(h)])
         if t == 0:
-            late_constants()
-            act(V("xb"), V("xr"), bias=128.0)
             spread_hold()
+            act(V("xb"), V("xr"), bias=128.0)
         else: gather_w("s", LAST)
         mm(V("PY", 256, 256 + NS), V("idn"), V("und"), True, True)
-        for lo, hi, pos, neg in ((0, C0, "idn", "idm"), (C0, NS, "idq", "idr")):
-            if lo < hi:
-                o = V("PC", 256 + lo, 256 + hi)
-                mm(o, V(pos), V("one", lo, hi), True, False)
-                mm(o, V(neg), V("und", lo, hi), False, False)
-                mm(o, V(neg), V("dead", lo, hi), False, True)
+        for (lo, hi), pos, neg in zip(CH, ("idq", "idn", "idq"), ("idr", "idm", "idr")):
+            o = V("PC", 256 + lo, 256 + hi)
+            mm(o, V(pos), V("one", lo, hi), True, False)
+            mm(o, V(neg), V("und", lo, hi), False, False)
+            mm(o, V(neg), V("dead", lo, hi), False, True)
         act(V("imp"), V("PC", 256, 256 + NS))
         act(V("PG", 256, 256 + NS), V(gs), bias=-2.0)
         if t == 0:
-            for c in range(LAST): gather_w("s", c)
-            gather_w("v", LAST)
-        for c in range(0 if t == 0 else 1, min(SCAN, LAST + 1)): diag(c)
+            constants_d()
+            gather_w("s", 0)
+            for c in (1, 2): gather_w("v", c)
+        diag(1)
         if t < RO - 1:
             mm(V("PC", 0, NS), V("one", 0, 128), V("dead"), True, True)
             op("s", lambda s: s.activation(T.cs[:], T.PC[:, 0:NS], F.Identity, accum_out=T.cf[:]), [R("PC", 0, NS)], [R("cs"), R("cf")])
-        tt(V("t3"), V("PY", 256, 256 + NS), V("ci"), A.mult)
-        if C0 < NS:
-            p = (16 * C0, NL)
-            op("v", lambda v: v.tensor_tensor_scan(T.sc[:, p[0]:p[1]], T.hold[:, p[0]:p[1]], T.W[:, p[0]:p[1]], 0.0, A.mult, A.min), [R("hold", *p), R("W", *p)], [R("sc", *p)])
+        tt(V("PQ", 256, 256 + NS), V("PY", 256, 256 + NS), V("ci"), A.mult)
+        scan(2048, 3072)
+        if t == 0: scan(0, 1024)
         tt(V("t1"), at(V("W"), V("idx", 0, 12)), V("dead"), A.mult)
-        tt(V("t4"), V("t1"), V("t3"), A.add)
-        if C0 < NS: tt(V("PA", 256 + C0, 256 + NS), step("sc", 16 * C0, NL, 15), V("imp", C0, NS), A.mult)
-        if C0 > 0: tt(V("PA", 256, 256 + C0), V("PA", 0, C0), V("imp", 0, C0), A.mult)
+        tt(V("t4"), V("PQ", 256, 256 + NS), V("t1"), A.add)
+        tt(V("PA", 256, 320), step("sc", 0, 1024, 15), V("imp", 0, 64), A.mult)
+        tt(V("PA", 384, 448), step("sc", 2048, 3072, 15), V("imp", 128, 192), A.mult)
+        tt(V("PA", 320, 384), V("PA", 64, 128), V("imp", 64, 128), A.mult)
         tt(V("ci"), V("PA", 256, 256 + NS), V("t4"), A.add)
         ts(V("k32"), V("ci"), 12, A.arith_shift_right)
         if t == RO - 1:
@@ -298,8 +304,7 @@ def rank_program(g, core, T, topo):
             dma("y", T.yg[:], T.kf[:], [R("kf")], [])
             cp(V("lf"), V("l32"))
             dma("y", T.yn[:], T.lf[:], [R("lf")], [])
-            tt(V("gm"), V("PG", 256, 256 + NS), V(h), A.min)
-            ts(V("yo"), V("gm"), float(2 - BIAS), A.add)
+            tt(V("yo"), V("PG", 256, 256 + NS), V(h), A.min)
             dma("y", T.yl[:], T.yo[:], [R("yo")], [])
             break
         ts(V("ku"), V("k32"), 3072.0, A.add)

import numpy as np
from concourse.mybir import AluOpType, ActivationFunctionType

A = AluOpType
F = ActivationFunctionType
RO = 4
NS = 192
NL = 3072
PAD = 3072
BIAS = 130
TOP = 12582912
CH = [(0, 64), (64, 128), (128, 192)]
LAST = len(CH) - 1
G_LANES, V_LANES = 4, 3

SCRATCH = {}


def _buf(where, dtype, **names):
    for name, cols in names.items(): SCRATCH[name] = (where, [128, cols], dtype)


_buf("sbuf", "bfloat16", gl=NS, xr=NL, xb=NL, gx=NL, D=2 * NL, ob=NL, ub=NL, yo=NS, dead=NS, und=NS, imp=NS, fi=NS, tr=NS, gm=NS, r16=16, tx=NS, half=NS,
     cs=NS, zo=144, zl=144, zq=144, idn=128, idm=128, id64=128, idq=128, idr=128, y1=128, y2=128, y3=128, ym=128, zz=128, one=NS, base=12)
_buf("sbuf", "float32", mf=4096, W=2 * NL, sc=NL, hold=NL, h16=16, h17=16, kf=NS, lf=NS, t1=NS, t4=NS, hh=NS, cf=1, th=1, jm=144, ln=16, kc=1, bc=12,
     b3=12, x1=12, x2=12, c15=1, c16=1, e15=1, me=1, w1=1, wl=1, wq=1, q1=1, q2=1, q3=1, k1=1, sv1=1, ek=2048, on16=16)
_buf("sbuf", "int32", gi=NS, ni=NS, mi=4096, ci=NS, k32=NS, l32=NS, c32=1, c33=1, pi=1, ka=1)
_buf("sbuf", "uint16", ku=NS, lu=NS, idx=16, li=16)
_buf("psum", "float32", PU=512, PO=512, PY=512, PL=512, PA=512, PQ=512, PC=512, PG=512)
for _t in range(RO): _buf("sbuf", "bfloat16", **{"gs%d" % _t: NS, "h%d" % _t: NS})
NDMA = 11
SEMAPHORES = ["sv", "ss", "sp", "sg", "snt"] + ["arr%d" % t for t in range(RO)] + ["dm%d" % i for i in range(NDMA)]


def rank_program(g, core, T, topo):
    rank = T.rank_of(core)
    if rank is None:
        return
    cores = list(T.cores)
    n = len(cores)
    S = T.sem
    queues = {"v": (g.vector, "sv"), "s": (g.scalar, "ss"), "p": (g.tensor, "sp"), "g": (g, "sg"), "y": (g.sync, None)}
    count = {"sv": 0, "ss": 0, "sp": 0, "sg": 0}
    seen = {}
    log = {}

    def need(q, sem, val):
        if seen.get((q, sem), 0) < val:
            queues[q][0].wait_ge(S[sem], val)
            seen[(q, sem)] = val

    def prep(q, reads, writes):
        todo = {}
        for wr, regs in ((False, reads), (True, writes)):
            for name, lo, hi in regs:
                bank = name in SCRATCH and SCRATCH[name][0] == "psum"
                for (w0, l0, h0, q0, sem0, val0) in log.get(name, []):
                    over = l0 < hi and lo < h0
                    if q0 == q: hit = (w0 or wr) and over and not (q == "p" and bank)
                    elif bank: hit = True
                    else: hit = (w0 or wr) and over
                    if hit: todo[sem0] = max(todo.get(sem0, 0), val0)
        for sem0 in sorted(todo): need(q, sem0, todo[sem0])

    def note(q, sem, val, reads, writes):
        for wr, regs in ((False, reads), (True, writes)):
            for name, lo, hi in regs:
                old = log.setdefault(name, [])
                old[:] = [e for e in old if not (lo <= e[1] and e[2] <= hi and (wr or (not e[0] and e[3] == q and e[4] == sem)))]
                old.append((wr, lo, hi, q, sem, val))

    def op(q, fn, reads, writes):
        prep(q, reads, writes)
        sem = queues[q][1]
        fn(queues[q][0]).then_inc(S[sem], 1)
        count[sem] += 1
        note(q, sem, count[sem], reads, writes)

    dmas = [0]

    def dma(q, out, in_, reads, writes):
        prep(q, reads, writes)
        sem = "dm%d" % dmas[0]
        dmas[0] += 1
        queues[q][0].dma_start(out, in_).then_inc(S[sem], 16)
        note("dma", sem, 16, reads, writes)

    def R(name, lo=0, hi=None): return (name, lo, SCRATCH[name][1][1] if hi is None and name in SCRATCH else hi)

    def V(name, lo=0, hi=None):
        r = R(name, lo, hi)
        return (T[name][:, r[1]:r[2]], [r])

    def step(name, lo, hi, first):
        return (T[name][:, lo + first:hi:16], [R(name, lo, hi)])

    def at(win, lst):
        return (win[0].indirect(lst[0]), win[1] + lst[1])

    def ts(out, in0, s1, op0, s2=None, op1=None):
        reads = list(in0[1])
        a, b = s1, s2
        if isinstance(s1, str): a, reads = T[s1][:], reads + [R(s1)]
        if isinstance(s2, str): b, reads = T[s2][:], reads + [R(s2)]
        if op1 is None: op("v", lambda v: v.tensor_scalar(out[0], in0[0], a, None, op0), reads, out[1])
        else: op("v", lambda v: v.tensor_scalar(out[0], in0[0], a, b, op0, op1), reads, out[1])

    def tt(out, a, b, f, lists=()): op("v", lambda v: v.tensor_tensor(out[0], a[0], b[0], f), a[1] + b[1] + list(lists), out[1])

    def cp(out, a): op("v", lambda v: v.tensor_copy(out[0], a[0]), a[1], out[1])

    def fill(out, c): op("v", lambda v: v.memset(out[0], c), [], out[1])

    def act(out, a, func=F.Identity, bias=0.0, scale=1.0): op("s", lambda s: s.activation(out[0], a[0], func, bias=bias, scale=scale), a[1], out[1])

    def mm(out, lhsT, rhs, start, stop): op("p", lambda p: p.matmul(out[0], lhsT[0], rhs[0], start, stop), lhsT[1] + rhs[1], out[1])

    def slide(name, k): return (T[name][:, 15 - k:143 - k], [R(name)])

    def lane_gx(q, k, src):
        o = T.gx[:, k::16]
        w = [("gx%d" % k, 0, NL)]
        if q == "v": op("v", lambda v: v.tensor_copy(o, src[0]), src[1], w)
        elif q == "s": op("s", lambda s: s.activation(o, src[0], F.Identity), src[1], w)
        else: op("g", lambda q: q.affine_select(o, src[0], [[0, NS]], A.is_gt, 0.0, 1, 0), src[1], w)

    GV = list(range(V_LANES))
    GG = list(range(V_LANES, V_LANES + G_LANES))
    GS = list(range(V_LANES + G_LANES, 16))

    dma("y", T.gl[:], T.lim[:], [], [R("gl")])
    dma("y", T.gi[:], T.grd[:], [], [R("gi")])
    dma("y", T.ni[:], T.nam[:], [], [R("ni")])
    dma("y", T.xr[:], T.xc[:], [], [R("xr")])
    QM = [(1024 * b, 1024 * b + 1024) for b in range(4)]
    for lo, hi in QM: dma("y", T.mi[:, lo:hi], T.rel[:, lo:hi], [], [R("mi", lo, hi)])

    IMP = {"allow_small_or_imprecise_dtypes": True}
    fill(V("on16"), 1.0)
    op("g", lambda q: q.iota(T.jm[:], [[1, 144]], 0, -1, **IMP), [], [R("jm")])
    op("g", lambda q: q.iota(T.pi[:], [[1, 1]], 0, 1), [], [R("pi")])
    op("g", lambda q: q.iota(T.bc[:], [[256, 12]], 0, 0, **IMP), [], [R("bc")])
    op("g", lambda q: q.iota(T.ln[:], [[1, 16]], 0, 0, **IMP), [], [R("ln")])
    for k in GG: lane_gx("g", k, V("gl"))
    op("g", lambda q: q.iota(T.ek[:], [[0, 2048]], 0, 0, **IMP), [], [R("ek")])
    for j in range(8):
        o = T.ek[:, 16 * j:16 * j + 1936:129]
        op("g", lambda q: q.affine_select(o, T.on16[:], [[-1, 16]], A.is_equal, 0.0, -16 * j, 1), [R("on16")], [R("ek")])
    for lo, hi in QM: op("g", lambda q: q.affine_select(T.mf[:, lo:hi], T.mi[:, lo:hi], [[0, 1024]], A.is_gt, 0.0, 1, 0), [R("mi", lo, hi)], [R("mf", lo, hi)])
    jm = V("jm", 0, 128)
    ts(V("ka"), V("pi"), 15, A.bitwise_and)
    cp(V("kc"), V("ka"))
    ts(V("c15"), V("kc"), -1.0, A.mult, 15.0, A.add)
    ts(V("zo"), V("jm"), "c15", A.is_equal)
    cp(V("ku"), V("gi"))
    fill(V("zz"), 0.0)
    ts(V("k1"), V("kc"), 1.0, A.add)
    ts(V("h16"), V("ln"), "k1", A.is_equal, 16777215.0, A.mult)
    ts(V("h17"), V("ln"), "kc", A.is_gt)
    tt(V("hold", 0, 16), V("h16"), V("h17"), A.add)
    cp(V("lu"), V("ni"))
    for k in GV: lane_gx("v", k, V("gl"))
    for k in GS: lane_gx("s", k, V("gl"))
    act(V("PG", 0, NS), V("gl"), bias=float(BIAS))
    for j in range(NL // NS): act(V("W", PAD + NS * j, PAD + NS * j + NS), V("gl"))
    act(V("D", PAD, 2 * NL), V("xr"), scale=0.0)
    ts(V("e15"), V("kc"), 15.0, A.is_equal)
    ts(V("c16"), V("c15"), 1.0, A.add)
    ts(V("me"), V("e15"), -1.0, A.mult)
    ts(V("w1"), V("e15"), float(PAD), A.mult)
    tt(V("wl"), V("w1"), V("c15"), A.subtract)
    ts(V("zl"), V("jm"), "c15", A.is_equal, "wl", A.mult)
    ts(V("idn"), jm, 0.0, A.is_equal)
    ts(V("id64"), jm, 0.0, A.is_equal, 64.0, A.mult)
    ts(V("y1"), jm, 0.0, A.is_gt)
    ts(V("y2"), jm, "c16", A.is_lt)
    tt(V("y3"), V("y1"), V("y2"), A.mult)
    ts(V("y1"), jm, 0.0, A.is_equal, "e15", A.mult)
    ts(V("y1"), V("y1"), -2.0, A.mult)
    tt(V("y2"), V("idn"), V("y1"), A.add)
    tt(V("ym"), V("y2"), V("y3"), A.subtract)
    ts(V("q1"), V("kc"), 16.0, A.mult)
    ts(V("base"), V("bc"), "q1", A.add)

    def constants_a():
        ts(V("sv1"), V("e15"), 2.0 ** 24 - 1.0, A.mult, 1.0, A.add)
        ts(V("sv1"), V("sv1"), 2.0 ** -24, A.mult)
        ts(V("idm"), jm, 0.0, A.is_equal, -1.0, A.mult)
        ts(V("idq"), jm, 0.0, A.is_equal, "sv1", A.mult)
        ts(V("idr"), V("idq"), -1.0, A.mult)

    def constants_b():
        fill(V("one"), 1.0)
        ts(V("k32"), V("gi"), 4096.0, A.mult, float(-TOP), A.add)

    def constants_c():
        tt(V("ci"), V("k32"), V("ni"), A.add)

    def constants_d():
        ts(V("q1"), V("kc"), 8.0, A.is_ge, -16.0, A.mult)
        ts(V("q2"), V("kc"), 2.0, A.mult, 1.0, A.add)
        tt(V("q2"), V("q2"), V("q1"), A.add)
        ts(V("q1"), V("q2"), 8.0, A.is_ge, -16.0, A.mult)
        tt(V("wq"), V("q2"), V("q1"), A.add)
        ts(V("zq"), V("jm"), "c15", A.is_equal, "wq", A.mult)
        ts(V("b3"), V("base"), 3072.0, A.add)
        fill(V("half"), 0.5)

    def spread_hold():
        for w in (16, 32, 64, 128, 256, 512): act(V("hold", w, 2 * w), V("hold", 0, w))

    def scan(lo, hi):
        op("v", lambda v: v.tensor_tensor_scan(T.sc[:, lo:hi], T.hold[:, 0:hi - lo], T.W[:, lo:hi], 0.0, A.mult, A.min), [R("hold", 0, hi - lo), R("W", lo, hi)], [R("sc", lo, hi)])

    def gather_w(q, c):
        a, b = CH[c]
        out, src = V("W", 16 * a, 16 * b), at(V("mf" if q == "s" else "mi"), V("lu", a, b))
        pad, first = (T.W[:, PAD + 15 + 16 * a:PAD + 16 * b:16], [R("W", PAD + 16 * a, PAD + 16 * b)]), step("W", 16 * a, 16 * b, 0)
        if q == "s":
            act(out, src, bias=float(-TOP))
            act(pad, first)
        else:
            ts(out, src, float(-TOP), A.add)
            cp(pad, first)

    def diag(c):
        a, b = CH[c]
        for k in range(16): mm(V("PA", a, b), V("ek", 128 * k, 128 * k + 128), step("W", 16 * a, 16 * b, k), k == 0, k == 15)

    def tally(dst, src, c, alone):
        a, b = CH[c]
        for k in range(16): mm(V(dst, a, b), slide("zo", k), step(src, 16 * a, 16 * b, k), alone and k == 0, alone and k == 15)

    for t in range(RO):
        X = V("xr") if t == 0 else V("xb")
        gs, h = "gs%d" % t, "h%d" % t
        mm(V("PU", 0, NS), V("zz"), V("gl"), True, False)
        for c, (a, b) in enumerate(CH):
            p = (16 * a, 16 * b)
            tt(V("D", *p), at(X, V("ku", a, b)), (T.gx[:, p[0]:p[1]], [("gx%d" % k, 0, NL) for k in range(16)]), A.subtract)
            ts(V("ob", *p), V("D", *p), 3.5, A.is_gt)
            if t > 0 and c < LAST: gather_w("s", c)
            act(V("ub", *p), V("D", *p), F.Sign, bias=0.5, scale=-1.0)
            tally("PO", "ob", c, True)
            if c == LAST and t > 0: act(V("PG", 0, NS), V("gm"), bias=2.0 if t < RO - 1 else 2.0 - 128)
            if c == LAST and t > 0:
                cp(V("c32"), V("cf"))
                ts(V("c33"), V("c32"), 1, A.bitwise_and)
                ts(V("th"), V("c33"), 5.0, A.add)
            if c == LAST and t == 0: constants_a()
            if c == LAST and t > 0: scan(0, 512)
            if c == LAST: ts(V("dead"), V("PO", 0, NS), "th" if t else 5.0, A.is_ge)
            if c == LAST and t == 0: constants_b()
            tally("PU", "ub", c, False)
        mm(V("PU", 0, NS), V("id64"), V("dead"), False, True)
        ts(V("und"), V("PU", 0, NS), 5.0, A.is_lt)
        mm(V("PL", 0, 12), V("idn"), V("base"), True, False)
        mm(V("PY", 0, NS), V("ym"), V("und"), True, True)
        ts(V("fi"), V("PY", 0, NS), "me", A.max, "e15", A.add)
        if t == 0: constants_c()
        for k in range(16): mm(V("PL", 0, 12), slide("zl", k), step("fi", 0, NS, k), False, k == 15)
        if t > 0: scan(512, 1024)
        ts(V("idx", 0, 12), V("PL", 0, 12), 15.0, A.add)
        ts(V("tr"), at(V("D"), V("idx", 0, 12)), 0.0, A.max)
        tt(V(gs), V("PG", 0, NS), V("tr"), A.add)
        dst, src = cores[(rank + 1 + t % (n - 1)) % n], cores[(rank - 1 - t % (n - 1)) % n]
        rid, pid, _ = topo.addr(dst)
        prep("g", [R(gs)], [])
        g.remote_dma(T[h][:], T[gs][:], S["arr%d" % t], S.snt, pid, rid, topo.mask(core, dst))
        note("remote", "arr%d" % t, len(topo.engines(src, core)), [], [R(h)])
        if t == 0:
            spread_hold()
            act(V("xb"), V("xr"), bias=128.0)
        else: gather_w("s", LAST)
        mm(V("PY", 256, 256 + NS), V("idn"), V("und"), True, True)
        for (lo, hi), pos, neg in zip(CH, ("idq", "idn", "idq"), ("idr", "idm", "idr")):
            o = V("PC", 256 + lo, 256 + hi)
            mm(o, V(pos), V("one", lo, hi), True, False)
            mm(o, V(neg), V("und", lo, hi), False, False)
            mm(o, V(neg), V("dead", lo, hi), False, True)
        act(V("imp"), V("PC", 256, 256 + NS))
        act(V("PG", 256, 256 + NS), V(gs), bias=-2.0)
        if t == 0:
            constants_d()
            gather_w("s", 0)
            for c in (1, 2): gather_w("v", c)
        diag(1)
        if t < RO - 1:
            mm(V("PC", 0, NS), V("one", 0, 128), V("dead"), True, True)
            op("s", lambda s: s.activation(T.cs[:], T.PC[:, 0:NS], F.Identity, accum_out=T.cf[:]), [R("PC", 0, NS)], [R("cs"), R("cf")])
        tt(V("PQ", 256, 256 + NS), V("PY", 256, 256 + NS), V("ci"), A.mult)
        scan(2048, 3072)
        if t == 0: scan(0, 1024)
        tt(V("t1"), at(V("W"), V("idx", 0, 12)), V("dead"), A.mult)
        tt(V("t4"), V("PQ", 256, 256 + NS), V("t1"), A.add)
        tt(V("PA", 256, 320), step("sc", 0, 1024, 15), V("imp", 0, 64), A.mult)
        tt(V("PA", 384, 448), step("sc", 2048, 3072, 15), V("imp", 128, 192), A.mult)
        tt(V("PA", 320, 384), V("PA", 64, 128), V("imp", 64, 128), A.mult)
        tt(V("ci"), V("PA", 256, 256 + NS), V("t4"), A.add)
        ts(V("k32"), V("ci"), 12, A.arith_shift_right)
        if t == RO - 1:
            ts(V("l32"), V("ci"), 4095, A.bitwise_and)
            ts(V("kf"), V("k32"), 3072.0, A.add)
            dma("y", T.yg[:], T.kf[:], [R("kf")], [])
            cp(V("lf"), V("l32"))
            dma("y", T.yn[:], T.lf[:], [R("lf")], [])
            tt(V("yo"), V("PG", 256, 256 + NS), V(h), A.min)
            dma("y", T.yl[:], T.yo[:], [R("yo")], [])
            break
        ts(V("ku"), V("k32"), 3072.0, A.add)
        tt(V("gm"), V("PG", 256, 256 + NS), V(h), A.min)
        act(V("hh"), V(h), bias=127.5 - BIAS)
        for k in range(16): mm(V("PQ", 0, 12), slide("zq", k), step(h, 0, NS, k), k == 0, k == 15)
        for k in GG: lane_gx("g", k, V("gm"))
        for k in GS: lane_gx("s", k, V("gm"))
        ts(V("l32"), V("ci"), 4095, A.bitwise_and)
        ts(V("r16", 0, 12), V("PQ", 0, 12), 3064.5, A.add)
        tt(V("x1"), V("PQ", 0, 12), V("r16", 0, 12), A.subtract)
        tt(V("x2"), V("x1"), V("b3"), A.add)
        cp(V("li", 0, 12), V("x2"))
        tt(V("tx"), at(V("xb"), V("li", 0, 12)), V("hh"), A.add)
        cp(V("lu"), V("l32"))
        for k in GV: lane_gx("v", k, V("gm"))
        out = at(V("xb"), V("li", 0, 12))
        tt((out[0], [R("xb")]), V("tx"), V("half"), A.mult, lists=[R("li", 0, 12)])

    g.wait_ge(S.snt, sum(len(topo.engines(core, cores[(rank + 1 + t % (n - 1)) % n])) for t in range(RO)))
    for sem in ("sv", "ss", "sp", "sg"): need("g", sem, count[sem])
    for i in range(dmas[0]): need("g", "dm%d" % i, 16)
